import numpy as np
import ml_dtypes


def mxq(x, axis, fmt="e4m3"):
    dtype, down = {"e4m3": (ml_dtypes.float8_e4m3fn, 7), "e5m2": (ml_dtypes.float8_e5m2, 14)}[fmt]
    v = np.moveaxis(np.asarray(x, np.float32).astype(ml_dtypes.bfloat16).astype(np.float64), axis, -1)
    blocks = v.reshape(v.shape[:-1] + (-1, 32))
    amax = np.abs(blocks).max(-1, keepdims=True)
    byte = np.maximum(np.where(amax > 0, np.frexp(amax)[1] - 1 + 127, 0) - down, 1)
    scale = np.exp2(byte - 127.0)
    codes = (blocks / scale).astype(np.float32).astype(dtype).astype(np.float64)
    return np.moveaxis((codes * scale).reshape(v.shape), -1, axis)


WIDE = False


def mx_kscale(k):
    if not WIDE:
        return np.ones(k)
    levels = np.array([10, -10, 5, -5, 0])
    if k % 512:
        return np.exp2(np.random.permutation(np.resize(levels, k // 32))).repeat(32)
    a = np.empty((k // 512, 16))
    for p in range(k // 512):
        a[p, :8] = np.random.permutation(np.resize(levels, 8))
        for g in range(8):
            far = levels[np.abs(levels - a[p, g]) >= 10]
            a[p, g + 8] = far[np.random.randint(len(far))]
    return np.exp2(a.ravel()).repeat(32)


def f64(x):
    return np.asarray(x).astype(np.float64)


def striped(idx):
    return np.tile(np.asarray(idx).reshape(-1, 16).T, (8, 1)).astype(np.uint16)


def unstriped(offs):
    return offs[:16].T.reshape(-1).astype(np.int64)


E2M1 = np.array([0.0, 0.5, 1.0, 1.5, 2.0, 3.0, 4.0, 6.0, -0.0, -0.5, -1.0, -1.5, -2.0, -3.0, -4.0, -6.0])


def pack_weight(w, fmt):
    k, n = w.shape
    w = f64(np.asarray(w, np.float32).astype(ml_dtypes.bfloat16)).reshape(k // 32, 32, n)
    amax = np.abs(w).max(1)
    if fmt == "e4m3":
        byte = np.frexp(amax)[1] - 1 + 127 - 7
    else:
        mant, ex = np.frexp(amax / 6.0)
        byte = np.where(mant > 0.5, ex, ex - 1) + 127
    byte = np.clip(np.where(amax > 0, byte, 1), 1, 254)
    scaled = (w * np.exp2(127.0 - byte)[:, None, :]).reshape(k, n).astype(np.float32)
    by_word = np.ascontiguousarray(scaled.reshape(k // 512, 128, 4, n).transpose(0, 1, 3, 2))
    if fmt == "e4m3":
        words = by_word.astype(ml_dtypes.float8_e4m3fn).view(np.uint8)
    else:
        c = by_word.astype(ml_dtypes.float4_e2m1fn).view(np.uint8) & 0xF
        words = (c[..., 0::2] | (c[..., 1::2] << 4)).reshape(k // 512, 128, 2 * n)
    return np.ascontiguousarray(words), np.ascontiguousarray(byte.astype(np.uint8).reshape(k // 512, 16, n))


def unpack_weight(words, scales, fmt):
    g, _, n = scales.shape
    words = np.ascontiguousarray(words).reshape(g, 128, n, -1)
    if fmt == "e4m3":
        vals = words.view(ml_dtypes.float8_e4m3fn).astype(np.float64)
    else:
        nib = np.empty((g, 128, n, 4), np.uint8)
        nib[..., 0::2] = words & 0xF
        nib[..., 1::2] = words >> 4
        vals = E2M1[nib]
    vals = vals * np.repeat(np.exp2(scales.astype(np.float64) - 127.0), 8, axis=1)[..., None]
    return vals.transpose(0, 1, 3, 2).reshape(g * 512, n)


K, R, F, T, J, M = 512, 128, 512, 2048, 512, 256


def setup_inputs():
    n = np.random.standard_normal
    idx = np.random.permutation(T)[:J]
    idx2 = np.random.permutation(J)[:M]
    idx3 = np.random.permutation(J)[:M]
    idx4 = np.random.permutation(J)[:M]
    fk = mx_kscale(K)
    ff = mx_kscale(F)
    tabp = pack_weight(n((K, T)) / fk[:, None], "e2m1")
    return {
        "tab_words": tabp[0],
        "tab_scales": tabp[1],
        "w1": (n((K, R)) * 1 / np.sqrt(K) * fk[:, None]).astype(np.float32),
        "temper": (np.random.uniform(0.6, 2.0, (R, 1))).astype(np.float32),
        "wo": (n((F, R)) * 1 / np.sqrt(F) * ff[:, None]).astype(np.float32),
        "dy": (n((F, M)) / ff[:, None]).astype(np.float32),
        "og": (np.random.uniform(0.3, 1.0, (R, 1))).astype(np.float32),
        "base": (0.3 * n((R, J))).astype(np.float32),
        "offs": striped(idx),
        "offs2": striped(idx2),
        "offs3": striped(idx3),
        "offs4": striped(idx4),
    }


def reference(tab_words, tab_scales, w1, temper, wo, dy, og, base, offs, offs2, offs3, offs4):
    idx = unstriped(offs)
    idx2 = unstriped(offs2)
    idx3 = unstriped(offs3)
    idx4 = unstriped(offs4)
    tabu = unpack_weight(tab_words, tab_scales, "e2m1")
    w1q = mxq(f64(w1), 0, "e4m3")
    tabidxg = tabu[:, idx]
    a = w1q.T @ tabidxg
    e1s = np.exp(a * f64(temper) * (-1.0))
    s = e1s[:, idx2] + e1s[:, idx3] + e1s[:, idx4]
    woq = mxq(f64(wo), 0, "e4m3")
    dyq = mxq(f64(dy), 0, "e4m3")
    c0 = woq.T @ dyq
    ds = c0 * (-1.0) / f64(temper) / s
    s1 = np.zeros((R, J))
    s1[:, idx2] = ds
    s2 = np.zeros((R, J))
    s2[:, idx3] = ds
    s3 = np.zeros((R, J))
    s3[:, idx4] = ds
    de1s = s1 + s2 + s3
    da = de1s * e1s * (-1.0) * f64(temper)
    hda = da * 2.0
    hde1s = hda * f64(temper) * (-1.0) * e1s
    hds = hde1s[:, idx4] + hde1s[:, idx3] + hde1s[:, idx2]
    hs = hds * c0 * (-1.0) / f64(temper) / np.square(s) * (-1.0)
    s51 = np.zeros((R, J))
    s51[:, idx2] = hs
    s52 = np.zeros((R, J))
    s52[:, idx3] = hs
    s53 = np.zeros((R, J))
    s53[:, idx4] = hs
    he1s = hda * f64(temper) * (-1.0) * de1s + s51 + s52 + s53
    ha = he1s * e1s * (-1.0) * f64(temper)
    y = ha * f64(og) + f64(base)
    return y

@@ -1,0 +1,225 @@
+from contextlib import ExitStack
+
+import concourse.mybir as mybir
+from concourse.masks import make_identity
+
+K, R, F, T, J, M = 512, 128, 512, 2048, 512, 256
+FLOPS = 2 * K * R * J + 2 * F * R * M
+
+F32 = mybir.dt.float32
+BF16 = mybir.dt.bfloat16
+I32 = mybir.dt.int32
+U32 = mybir.dt.uint32
+U16 = mybir.dt.uint16
+U8 = mybir.dt.uint8
+FP8X4 = mybir.dt.float8_e4m3fn_x4
+FP4X4 = mybir.dt.float4_e2m1fn_x4
+ACT = mybir.ActivationFunctionType
+MULT = mybir.AluOpType.mult
+ADD = mybir.AluOpType.add
+
+P = 128
+PACK = 4
+GROUP = 16
+HALF_J = J // 2
+HALF_M = M // 2
+
+
+def load_rows(nc, pool, rows, name):
+    raw = pool.tile([P, PACK, rows.shape[1]], F32, name=name)
+    nc.sync.dma_start(out=raw[:], in_=rows.rearrange("(p t) c -> p t c", t=PACK))
+    return raw
+
+
+def interleave_views(pool, raw, name):
+    width = raw.shape[2]
+    grouped = pool.tile([P, width, PACK], BF16, name=name, align_bytes=64)
+    dst = grouped[:].rearrange("p (c i) t -> p c t i", i=4)
+    src = raw[:].rearrange("p t (c i) -> p c t i", i=4)
+    return grouped, dst, src
+
+
+def quantize(nc, pool, grouped, name):
+    width = grouped.shape[1]
+    codes = pool.tile([P, width], U32, name=name + "_codes", align_bytes=64)
+    scales = pool.tile([P, width], U8, name=name + "_scales", align_bytes=64)
+    nc.vector.quantize_mx(
+        out=codes[:].bitcast(FP8X4),
+        scales=scales[:],
+        in_=grouped[:].rearrange("p c t -> p (c t)"),
+    )
+    return codes, scales
+
+
+def tile_attend_gpcsoftleast_kernel(
+    tc, tab_words, tab_scales, w1, temper, wo, dy, og, base, offs, offs2, offs3, offs4, out
+):
+    nc = tc.nc
+    with ExitStack() as ctx:
+        sb = ctx.enter_context(tc.tile_pool(name="sb", bufs=1))
+        ps = ctx.enter_context(tc.psum_pool(name="ps", bufs=1))
+
+        table_scales = sb.tile([P, T], U8, name="table_scales", align_bytes=64)
+        nc.vector.memset(table_scales[:].bitcast(I32), 0)
+
+        slots = sb.tile([P, J // GROUP], U16, name="slots")
+        nc.sync.dma_start(slots[:], offs)
+        w1_raw = load_rows(nc, sb, w1, "w1_raw")
+        for quad in range(4):
+            nc.sync.dma_start(
+                out=table_scales[32 * quad : 32 * quad + 4, :].bitcast(I32),
+                in_=tab_scales[0, 4 * quad : 4 * quad + 4, :].bitcast(I32),
+            )
+        table_words = sb.tile([P, T], U16, name="table_words", align_bytes=64)
+        nc.sync.dma_start(out=table_words[:].bitcast(I32), in_=tab_words[0].bitcast(I32))
+        temper_sb = sb.tile([P, 1], F32, name="temper_sb")
+        nc.sync.dma_start(out=temper_sb[:], in_=temper)
+        wo_raw = load_rows(nc, sb, wo, "wo_raw")
+        dy_raw = load_rows(nc, sb, dy, "dy_raw")
+        picks = []
+        for n, source in enumerate((offs2, offs3, offs4)):
+            pick = sb.tile([P, M // GROUP], U16, name=f"pick{n}")
+            nc.sync.dma_start(pick[:], source)
+            picks.append(pick)
+        og_sb = sb.tile([P, 1], F32, name="og_sb")
+        nc.sync.dma_start(out=og_sb[:], in_=og)
+        base_sb = sb.tile([P, J], F32, name="base_sb")
+        nc.sync.dma_start(out=base_sb[:], in_=base)
+
+        ident = sb.tile([P, P], F32, name="ident")
+        make_identity(nc, ident[:])
+
+        windows = []
+        for n in range(3):
+            window = sb.tile([P, J], F32, name=f"window{n}")
+            nc.vector.memset(window[:], 0.0)
+            windows.append(window)
+
+        w1_grouped, dst, src = interleave_views(sb, w1_raw, "w1_grouped")
+        nc.scalar.activation(dst, src, ACT.Copy)
+        neg_t = sb.tile([P, 1], F32, name="neg_t")
+        nc.scalar.activation(neg_t[:], temper_sb[:], ACT.Copy, scale=-1.0)
+        slot_scales = sb.tile([P, J], U8, name="slot_scales", align_bytes=64)
+        nc.vector.tensor_copy(slot_scales[:], table_scales[:].indirect(slots[:]))
+        w1_codes, w1_scales = quantize(nc, sb, w1_grouped, "w1")
+        wo_grouped, dst, src = interleave_views(sb, wo_raw, "wo_grouped")
+        nc.scalar.activation(dst, src, ACT.Copy)
+
+        e = sb.tile([P, J], F32, name="e")
+        for h in range(2):
+            cols = slice(h * HALF_J, (h + 1) * HALF_J)
+            entries = slice(h * HALF_J // GROUP, (h + 1) * HALF_J // GROUP)
+            slot_words = sb.tile([P, HALF_J], U16, name=f"slot_words{h}", align_bytes=64)
+            nc.vector.tensor_copy(slot_words[:], table_words[:].indirect(slots[:, entries]))
+            a_ps = ps.tile([P, HALF_J], F32, name=f"a_ps{h}")
+            nc.tensor.matmul_mx(
+                out=a_ps[:],
+                lhsT=w1_codes[:].bitcast(FP8X4),
+                lhsT_scale=w1_scales[:],
+                rhs=slot_words[:].bitcast(FP4X4),
+                rhs_scale=slot_scales[:, cols],
+                start=True,
+                stop=True,
+            )
+            nc.scalar.activation(e[:, cols], a_ps[:], ACT.Exp, scale=neg_t[:])
+
+        dy_grouped, dst, src = interleave_views(sb, dy_raw, "dy_grouped")
+        nc.vector.tensor_copy(dst, src)
+        wo_codes, wo_scales = quantize(nc, sb, wo_grouped, "wo")
+        dy_codes, dy_scales = quantize(nc, sb, dy_grouped, "dy")
+        c0_ps = ps.tile([P, M], F32, name="c0_ps")
+        nc.tensor.matmul_mx(
+            out=c0_ps[:],
+            lhsT=wo_codes[:].bitcast(FP8X4),
+            lhsT_scale=wo_scales[:],
+            rhs=dy_codes[:].bitcast(FP8X4),
+            rhs_scale=dy_scales[:],
+            start=True,
+            stop=True,
+        )
+
+        halves = [
+            (slice(h * HALF_M, (h + 1) * HALF_M), slice(h * HALF_M // GROUP, (h + 1) * HALF_M // GROUP))
+            for h in range(2)
+        ]
+        e_picked = [sb.tile([P, M], F32, name=f"e_picked{n}") for n in range(3)]
+        s_part = sb.tile([P, M], F32, name="s_part")
+        s = sb.tile([P, M], F32, name="s")
+        root = sb.tile([P, M], F32, name="root")
+        inv_s = sb.tile([P, M], F32, name="inv_s")
+        for cols, entries in halves:
+            for n in range(3):
+                nc.vector.tensor_copy(e_picked[n][:, cols], e[:].indirect(picks[n][:, entries]))
+            nc.vector.tensor_tensor(s_part[:, cols], e_picked[0][:, cols], e_picked[1][:, cols], ADD)
+            nc.vector.tensor_tensor(s[:, cols], s_part[:, cols], e_picked[2][:, cols], ADD)
+            nc.scalar.activation(root[:, cols], s[:, cols], ACT.Abs_reciprocal_sqrt)
+            nc.scalar.activation(inv_s[:, cols], root[:, cols], ACT.Square)
+
+        neg_2t = sb.tile([P, 1], F32, name="neg_2t")
+        nc.scalar.activation(neg_2t[:], temper_sb[:], ACT.Copy, scale=-2.0)
+        neg_og = sb.tile([P, 1], F32, name="neg_og")
+        nc.scalar.activation(neg_og[:], og_sb[:], ACT.Copy, scale=-1.0)
+        neg_2t_og = sb.tile([P, 1], F32, name="neg_2t_og")
+        nc.scalar.activation(neg_2t_og[:], og_sb[:], ACT.Copy, scale=neg_2t[:])
+
+        q = sb.tile([P, M], F32, name="q")
+        for cols, entries in halves:
+            nc.vector.tensor_tensor(q[:, cols], c0_ps[:, cols], inv_s[:, cols], MULT)
+            nc.vector.tensor_tensor(
+                windows[0][:].indirect(picks[0][:, entries]), q[:, cols], e_picked[0][:, cols], MULT
+            )
+        for n in (1, 2):
+            nc.vector.tensor_tensor(windows[n][:].indirect(picks[n][:]), q[:], e_picked[n][:], MULT)
+
+        slot_halves = [slice(h * HALF_J, (h + 1) * HALF_J) for h in range(2)]
+        da_part = sb.tile([P, J], F32, name="da_part")
+        da = sb.tile([P, J], F32, name="da")
+        hde = sb.tile([P, J], F32, name="hde")
+        for cols in slot_halves:
+            nc.vector.tensor_tensor(da_part[:, cols], windows[0][:, cols], windows[1][:, cols], ADD)
+        for cols in slot_halves:
+            nc.vector.tensor_tensor(da[:, cols], da_part[:, cols], windows[2][:, cols], ADD)
+        for cols in slot_halves:
+            nc.vector.scalar_tensor_tensor(hde[:, cols], da[:, cols], neg_2t[:], e[:, cols], MULT, MULT)
+        u = sb.tile([P, M], F32, name="u")
+        nc.vector.tensor_tensor(u[:], q[:], inv_s[:], MULT)
+
+        da_sq = sb.tile([P, J], F32, name="da_sq")
+        nc.scalar.activation(da_sq[:], da[:], ACT.Square)
+        direct = sb.tile([P, J], F32, name="direct")
+        nc.scalar.activation(direct[:], da_sq[:], ACT.Copy, scale=neg_2t_og[:])
+
+        h_picked = [sb.tile([P, M], F32, name=f"h_picked{n}") for n in range(3)]
+        for n in range(3):
+            nc.vector.tensor_copy(h_picked[n][:], hde[:].indirect(picks[n][:]))
+        hds_part = sb.tile([P, M], F32, name="hds_part")
+        hds = sb.tile([P, M], F32, name="hds")
+        hs = sb.tile([P, M], F32, name="hs")
+        nc.vector.tensor_tensor(hds_part[:], h_picked[0][:], h_picked[1][:], ADD)
+        for cols, entries in halves:
+            nc.vector.tensor_tensor(hds[:, cols], hds_part[:, cols], h_picked[2][:, cols], ADD)
+        for cols, entries in halves:
+            nc.vector.scalar_tensor_tensor(hs[:, cols], hds[:, cols], neg_og[:], u[:, cols], MULT, MULT)
+        for n in range(3):
+            nc.vector.tensor_tensor(windows[n][:].indirect(picks[n][:]), hs[:], e_picked[n][:], MULT)
+
+        turned = sb.tile([P, J], F32, name="turned")
+        back_ps = ps.tile([P, J], F32, name="back_ps")
+        addends = (base_sb, direct, windows[0])
+        for b in range(J // P):
+            cols = slice(b * P, (b + 1) * P)
+            sum_ps = ps.tile([P, P], F32, name=f"sum_ps{b}")
+            for n, addend in enumerate(addends):
+                nc.tensor.matmul(
+                    sum_ps[:], addend[:, cols], ident[:], start=(n == 0), stop=(n == 2), is_transpose=True
+                )
+            nc.scalar.copy(turned[:, cols], sum_ps[:])
+            nc.tensor.transpose(back_ps[:, cols], turned[:, cols], ident[:])
+
+        result_part = sb.tile([P, J], F32, name="result_part")
+        for cols in slot_halves:
+            nc.vector.tensor_tensor(result_part[:, cols], back_ps[:, cols], windows[1][:, cols], ADD)
+        for h, cols in enumerate(slot_halves):
+            result = sb.tile([P, HALF_J], F32, name=f"result{h}")
+            nc.vector.tensor_tensor(result[:], result_part[:, cols], windows[2][:, cols], ADD)
+            (nc.sync, nc.scalar)[h].dma_start(out=out[:, cols], in_=result[:])

@@ -33,7 +33,7 @@ def load_rows(nc, pool, rows, name):
 
 def interleave_views(pool, raw, name):
     width = raw.shape[2]
-    grouped = pool.tile([P, width, PACK], BF16, name=name, align_bytes=64)
+    grouped = pool.tile([P, width, PACK], BF16, name=name, tag=name, align_bytes=64)
     dst = grouped[:].rearrange("p (c i) t -> p c t i", i=4)
     src = raw[:].rearrange("p t (c i) -> p c t i", i=4)
     return grouped, dst, src
@@ -62,6 +62,8 @@ def tile_attend_gpcsoftleast_kernel(
         table_scales = sb.tile([P, T], U8, name="table_scales", align_bytes=64)
         nc.vector.memset(table_scales[:].bitcast(I32), 0)
 
+        table_words = sb.tile([P, T], U16, name="table_words", align_bytes=64)
+        nc.sync.dma_start(out=table_words[:].bitcast(I32), in_=tab_words[0].bitcast(I32))
         slots = sb.tile([P, J // GROUP], U16, name="slots")
         nc.sync.dma_start(slots[:], offs)
         w1_raw = load_rows(nc, sb, w1, "w1_raw")
@@ -70,10 +72,8 @@ def tile_attend_gpcsoftleast_kernel(
                 out=table_scales[32 * quad : 32 * quad + 4, :].bitcast(I32),
                 in_=tab_scales[0, 4 * quad : 4 * quad + 4, :].bitcast(I32),
             )
-        table_words = sb.tile([P, T], U16, name="table_words", align_bytes=64)
-        nc.sync.dma_start(out=table_words[:].bitcast(I32), in_=tab_words[0].bitcast(I32))
         temper_sb = sb.tile([P, 1], F32, name="temper_sb")
-        nc.sync.dma_start(out=temper_sb[:], in_=temper)
+        nc.gpsimd.dma_start(out=temper_sb[:], in_=temper)
         wo_raw = load_rows(nc, sb, wo, "wo_raw")
         dy_raw = load_rows(nc, sb, dy, "dy_raw")
         picks = []
@@ -82,7 +82,7 @@ def tile_attend_gpcsoftleast_kernel(
             nc.sync.dma_start(pick[:], source)
             picks.append(pick)
         og_sb = sb.tile([P, 1], F32, name="og_sb")
-        nc.sync.dma_start(out=og_sb[:], in_=og)
+        nc.gpsimd.dma_start(out=og_sb[:], in_=og)
         base_sb = sb.tile([P, J], F32, name="base_sb")
         nc.sync.dma_start(out=base_sb[:], in_=base)
 
@@ -96,32 +96,31 @@ def tile_attend_gpcsoftleast_kernel(
             windows.append(window)
 
         w1_grouped, dst, src = interleave_views(sb, w1_raw, "w1_grouped")
-        nc.scalar.activation(dst, src, ACT.Copy)
-        neg_t = sb.tile([P, 1], F32, name="neg_t")
-        nc.scalar.activation(neg_t[:], temper_sb[:], ACT.Copy, scale=-1.0)
-        slot_scales = sb.tile([P, J], U8, name="slot_scales", align_bytes=64)
-        nc.vector.tensor_copy(slot_scales[:], table_scales[:].indirect(slots[:]))
+        nc.scalar.activation(dst, src, ACT.Copy, scale=-1.0)
+        slot_words = sb.tile([P, J], U16, name="slot_words", align_bytes=64)
+        nc.vector.tensor_copy(slot_words[:], table_words[:].indirect(slots[:]))
         w1_codes, w1_scales = quantize(nc, sb, w1_grouped, "w1")
         wo_grouped, dst, src = interleave_views(sb, wo_raw, "wo_grouped")
         nc.scalar.activation(dst, src, ACT.Copy)
 
         e = sb.tile([P, J], F32, name="e")
         for h in range(2):
-            cols = slice(h * HALF_J, (h + 1) * HALF_J)
             entries = slice(h * HALF_J // GROUP, (h + 1) * HALF_J // GROUP)
-            slot_words = sb.tile([P, HALF_J], U16, name=f"slot_words{h}", align_bytes=64)
-            nc.vector.tensor_copy(slot_words[:], table_words[:].indirect(slots[:, entries]))
-            a_ps = ps.tile([P, HALF_J], F32, name=f"a_ps{h}")
-            nc.tensor.matmul_mx(
-                out=a_ps[:],
-                lhsT=w1_codes[:].bitcast(FP8X4),
-                lhsT_scale=w1_scales[:],
-                rhs=slot_words[:].bitcast(FP4X4),
-                rhs_scale=slot_scales[:, cols],
-                start=True,
-                stop=True,
-            )
-            nc.scalar.activation(e[:, cols], a_ps[:], ACT.Exp, scale=neg_t[:])
+            slot_scales = sb.tile([P, HALF_J], U8, name=f"slot_scales{h}", align_bytes=64)
+            nc.vector.tensor_copy(slot_scales[:], table_scales[:].indirect(slots[:, entries]))
+            for b in range(2 * h, 2 * h + 2):
+                cols = slice(b * P, (b + 1) * P)
+                a_ps = ps.tile([P, P], F32, name=f"a_ps{b}", tag=f"block{b}")
+                nc.tensor.matmul_mx(
+                    out=a_ps[:],
+                    lhsT=w1_codes[:].bitcast(FP8X4),
+                    lhsT_scale=w1_scales[:],
+                    rhs=slot_words[:, cols].bitcast(FP4X4),
+                    rhs_scale=slot_scales[:, (b % 2) * P : (b % 2 + 1) * P],
+                    start=True,
+                    stop=True,
+                )
+                nc.scalar.activation(e[:, cols], a_ps[:], ACT.Exp, scale=temper_sb[:])
 
         dy_grouped, dst, src = interleave_views(sb, dy_raw, "dy_grouped")
         nc.vector.tensor_copy(dst, src)
@@ -142,84 +141,90 @@ def tile_attend_gpcsoftleast_kernel(
             (slice(h * HALF_M, (h + 1) * HALF_M), slice(h * HALF_M // GROUP, (h + 1) * HALF_M // GROUP))
             for h in range(2)
         ]
-        e_picked = [sb.tile([P, M], F32, name=f"e_picked{n}") for n in range(3)]
-        s_part = sb.tile([P, M], F32, name="s_part")
+        e_picked_all = sb.tile([P, 3 * M], F32, name="e_picked", tag="dy_grouped", align_bytes=64)
+        e_picked = [e_picked_all[:, n * M : (n + 1) * M] for n in range(3)]
+        s_part = sb.tile([P, M], F32, name="s_part", tag="s_part")
         s = sb.tile([P, M], F32, name="s")
         root = sb.tile([P, M], F32, name="root")
         inv_s = sb.tile([P, M], F32, name="inv_s")
+        for n in range(3):
+            nc.vector.tensor_copy(e_picked[n], e[:].indirect(picks[n][:]))
         for cols, entries in halves:
-            for n in range(3):
-                nc.vector.tensor_copy(e_picked[n][:, cols], e[:].indirect(picks[n][:, entries]))
             nc.vector.tensor_tensor(s_part[:, cols], e_picked[0][:, cols], e_picked[1][:, cols], ADD)
+        for cols, entries in halves:
             nc.vector.tensor_tensor(s[:, cols], s_part[:, cols], e_picked[2][:, cols], ADD)
             nc.scalar.activation(root[:, cols], s[:, cols], ACT.Abs_reciprocal_sqrt)
             nc.scalar.activation(inv_s[:, cols], root[:, cols], ACT.Square)
+        c0_e = sb.tile([P, M], F32, name="c0_e", tag="s_part")
+        nc.vector.scalar_tensor_tensor(c0_e[:], c0_ps[:], -2.0, e_picked[0], MULT, MULT)
 
-        neg_2t = sb.tile([P, 1], F32, name="neg_2t")
-        nc.scalar.activation(neg_2t[:], temper_sb[:], ACT.Copy, scale=-2.0)
-        neg_og = sb.tile([P, 1], F32, name="neg_og")
-        nc.scalar.activation(neg_og[:], og_sb[:], ACT.Copy, scale=-1.0)
-        neg_2t_og = sb.tile([P, 1], F32, name="neg_2t_og")
-        nc.scalar.activation(neg_2t_og[:], og_sb[:], ACT.Copy, scale=neg_2t[:])
+        direct_gain = sb.tile([P, 1], F32, name="direct_gain")
+        nc.gpsimd.tensor_scalar(direct_gain[:], og_sb[:], temper_sb[:], -0.5, MULT, MULT)
+
+        def add_on_tensor_engine(addends, name):
+            turned = sb.tile([P, J], F32, name=name + "_turned")
+            back = [ps.tile([P, HALF_J], F32, name=f"{name}_back{h}", tag=f"half{h}") for h in range(2)]
+            blocks = [slice(b * P, (b + 1) * P) for b in range(J // P)]
+            sums = [ps.tile([P, P], F32, name=f"{name}_sum{b}", tag=f"block{b}") for b in range(J // P)]
+            for n, addend in enumerate(addends):
+                for b, cols in enumerate(blocks):
+                    nc.tensor.matmul(
+                        sums[b][:],
+                        addend[:, cols],
+                        ident[:],
+                        start=(n == 0),
+                        stop=(n == len(addends) - 1),
+                        is_transpose=True,
+                    )
+            for b, cols in enumerate(blocks):
+                nc.scalar.copy(turned[:, cols], sums[b][:])
+                nc.tensor.transpose(back[b // 2][:, (b % 2) * P : (b % 2 + 1) * P], turned[:, cols], ident[:])
+            return back
 
         q = sb.tile([P, M], F32, name="q")
-        for cols, entries in halves:
-            nc.vector.tensor_tensor(q[:, cols], c0_ps[:, cols], inv_s[:, cols], MULT)
-            nc.vector.tensor_tensor(
-                windows[0][:].indirect(picks[0][:, entries]), q[:, cols], e_picked[0][:, cols], MULT
-            )
+        for h, (cols, entries) in enumerate(halves):
+            if h == 1:
+                nc.vector.scalar_tensor_tensor(q[:], c0_ps[:], -2.0, inv_s[:], MULT, MULT)
+            nc.vector.tensor_tensor(windows[0][:].indirect(picks[0][:, entries]), c0_e[:, cols], inv_s[:, cols], MULT)
         for n in (1, 2):
-            nc.vector.tensor_tensor(windows[n][:].indirect(picks[n][:]), q[:], e_picked[n][:], MULT)
+            nc.vector.tensor_tensor(windows[n][:].indirect(picks[n][:]), q[:], e_picked[n], MULT)
+        u = sb.tile([P, M], F32, name="u")
+        nc.vector.scalar_tensor_tensor(u[:], q[:], 0.5, inv_s[:], MULT, MULT)
 
         slot_halves = [slice(h * HALF_J, (h + 1) * HALF_J) for h in range(2)]
-        da_part = sb.tile([P, J], F32, name="da_part")
-        da = sb.tile([P, J], F32, name="da")
+        first_two = add_on_tensor_engine(windows[:2], "first")
+        neg_hda = sb.tile([P, J], F32, name="neg_hda")
         hde = sb.tile([P, J], F32, name="hde")
+        for h, cols in enumerate(slot_halves):
+            nc.vector.tensor_tensor(neg_hda[:, cols], first_two[h][:], windows[2][:, cols], ADD)
         for cols in slot_halves:
-            nc.vector.tensor_tensor(da_part[:, cols], windows[0][:, cols], windows[1][:, cols], ADD)
-        for cols in slot_halves:
-            nc.vector.tensor_tensor(da[:, cols], da_part[:, cols], windows[2][:, cols], ADD)
-        for cols in slot_halves:
-            nc.vector.scalar_tensor_tensor(hde[:, cols], da[:, cols], neg_2t[:], e[:, cols], MULT, MULT)
-        u = sb.tile([P, M], F32, name="u")
-        nc.vector.tensor_tensor(u[:], q[:], inv_s[:], MULT)
+            nc.vector.scalar_tensor_tensor(hde[:, cols], neg_hda[:, cols], temper_sb[:], e[:, cols], MULT, MULT)
 
-        da_sq = sb.tile([P, J], F32, name="da_sq")
-        nc.scalar.activation(da_sq[:], da[:], ACT.Square)
+        hda_sq = sb.tile([P, J], F32, name="hda_sq")
+        nc.scalar.activation(hda_sq[:], neg_hda[:], ACT.Square)
         direct = sb.tile([P, J], F32, name="direct")
-        nc.scalar.activation(direct[:], da_sq[:], ACT.Copy, scale=neg_2t_og[:])
+        nc.scalar.activation(direct[:], hda_sq[:], ACT.Copy, scale=direct_gain[:])
 
-        h_picked = [sb.tile([P, M], F32, name=f"h_picked{n}") for n in range(3)]
-        for n in range(3):
-            nc.vector.tensor_copy(h_picked[n][:], hde[:].indirect(picks[n][:]))
-        hds_part = sb.tile([P, M], F32, name="hds_part")
-        hds = sb.tile([P, M], F32, name="hds")
-        hs = sb.tile([P, M], F32, name="hs")
-        nc.vector.tensor_tensor(hds_part[:], h_picked[0][:], h_picked[1][:], ADD)
+        running = [sb.tile([P, M], F32, name=f"hds{n}") for n in range(3)]
         for cols, entries in halves:
-            nc.vector.tensor_tensor(hds[:, cols], hds_part[:, cols], h_picked[2][:, cols], ADD)
-        for cols, entries in halves:
-            nc.vector.scalar_tensor_tensor(hs[:, cols], hds[:, cols], neg_og[:], u[:, cols], MULT, MULT)
-        for n in range(3):
-            nc.vector.tensor_tensor(windows[n][:].indirect(picks[n][:]), hs[:], e_picked[n][:], MULT)
-
-        turned = sb.tile([P, J], F32, name="turned")
-        back_ps = ps.tile([P, J], F32, name="back_ps")
-        addends = (base_sb, direct, windows[0])
-        for b in range(J // P):
-            cols = slice(b * P, (b + 1) * P)
-            sum_ps = ps.tile([P, P], F32, name=f"sum_ps{b}")
-            for n, addend in enumerate(addends):
-                nc.tensor.matmul(
-                    sum_ps[:], addend[:, cols], ident[:], start=(n == 0), stop=(n == 2), is_transpose=True
+            nc.vector.tensor_copy(running[0][:, cols], hde[:].indirect(picks[0][:, entries]))
+        for n in (1, 2):
+            for cols, entries in halves:
+                nc.vector.tensor_tensor(
+                    running[n][:, cols], hde[:].indirect(picks[n][:, entries]), running[n - 1][:, cols], ADD
                 )
-            nc.scalar.copy(turned[:, cols], sum_ps[:])
-            nc.tensor.transpose(back_ps[:, cols], turned[:, cols], ident[:])
+        hs = sb.tile([P, M], F32, name="hs")
+        for cols, entries in halves:
+            nc.vector.scalar_tensor_tensor(hs[:, cols], running[2][:, cols], og_sb[:], u[:, cols], MULT, MULT)
+        for cols, entries in halves:
+            nc.vector.tensor_tensor(
+                windows[0][:].indirect(picks[0][:, entries]), hs[:, cols], e_picked[0][:, cols], MULT
+            )
+        for n in (1, 2):
+            nc.vector.tensor_tensor(windows[n][:].indirect(picks[n][:]), hs[:], e_picked[n], MULT)
 
-        result_part = sb.tile([P, J], F32, name="result_part")
-        for cols in slot_halves:
-            nc.vector.tensor_tensor(result_part[:, cols], back_ps[:, cols], windows[1][:, cols], ADD)
+        rest = add_on_tensor_engine((base_sb, direct, windows[0], windows[1]), "last")
         for h, cols in enumerate(slot_halves):
             result = sb.tile([P, HALF_J], F32, name=f"result{h}")
-            nc.vector.tensor_tensor(result[:], result_part[:, cols], windows[2][:, cols], ADD)
+            nc.vector.tensor_tensor(result[:], rest[h][:], windows[2][:, cols], ADD)
             (nc.sync, nc.scalar)[h].dma_start(out=out[:, cols], in_=result[:])

from contextlib import ExitStack

import concourse.mybir as mybir
from concourse.masks import make_identity

K, R, F, T, J, M = 512, 128, 512, 2048, 512, 256
FLOPS = 2 * K * R * J + 2 * F * R * M

F32 = mybir.dt.float32
BF16 = mybir.dt.bfloat16
I32 = mybir.dt.int32
U32 = mybir.dt.uint32
U16 = mybir.dt.uint16
U8 = mybir.dt.uint8
FP8X4 = mybir.dt.float8_e4m3fn_x4
FP4X4 = mybir.dt.float4_e2m1fn_x4
ACT = mybir.ActivationFunctionType
MULT = mybir.AluOpType.mult
ADD = mybir.AluOpType.add

P = 128
PACK = 4
GROUP = 16
HALF_J = J // 2
HALF_M = M // 2


def load_rows(nc, pool, rows, name):
    raw = pool.tile([P, PACK, rows.shape[1]], F32, name=name)
    nc.sync.dma_start(out=raw[:], in_=rows.rearrange("(p t) c -> p t c", t=PACK))
    return raw


def interleave_views(pool, raw, name):
    width = raw.shape[2]
    grouped = pool.tile([P, width, PACK], BF16, name=name, tag=name, align_bytes=64)
    dst = grouped[:].rearrange("p (c i) t -> p c t i", i=4)
    src = raw[:].rearrange("p t (c i) -> p c t i", i=4)
    return grouped, dst, src


def quantize(nc, pool, grouped, name):
    width = grouped.shape[1]
    codes = pool.tile([P, width], U32, name=name + "_codes", align_bytes=64)
    scales = pool.tile([P, width], U8, name=name + "_scales", align_bytes=64)
    nc.vector.quantize_mx(
        out=codes[:].bitcast(FP8X4),
        scales=scales[:],
        in_=grouped[:].rearrange("p c t -> p (c t)"),
    )
    return codes, scales


def tile_attend_gpcsoftleast_kernel(
    tc, tab_words, tab_scales, w1, temper, wo, dy, og, base, offs, offs2, offs3, offs4, out
):
    nc = tc.nc
    with ExitStack() as ctx:
        sb = ctx.enter_context(tc.tile_pool(name="sb", bufs=1))
        ps = ctx.enter_context(tc.psum_pool(name="ps", bufs=1))

        table_scales = sb.tile([P, T], U8, name="table_scales", align_bytes=64)
        nc.vector.memset(table_scales[:].bitcast(I32), 0)

        table_words = sb.tile([P, T], U16, name="table_words", align_bytes=64)
        nc.sync.dma_start(out=table_words[:].bitcast(I32), in_=tab_words[0].bitcast(I32))
        slots = sb.tile([P, J // GROUP], U16, name="slots")
        nc.sync.dma_start(slots[:], offs)
        w1_raw = load_rows(nc, sb, w1, "w1_raw")
        for quad in range(4):
            nc.sync.dma_start(
                out=table_scales[32 * quad : 32 * quad + 4, :].bitcast(I32),
                in_=tab_scales[0, 4 * quad : 4 * quad + 4, :].bitcast(I32),
            )
        temper_sb = sb.tile([P, 1], F32, name="temper_sb")
        nc.gpsimd.dma_start(out=temper_sb[:], in_=temper)
        wo_raw = load_rows(nc, sb, wo, "wo_raw")
        dy_raw = load_rows(nc, sb, dy, "dy_raw")
        picks = []
        for n, source in enumerate((offs2, offs3, offs4)):
            pick = sb.tile([P, M // GROUP], U16, name=f"pick{n}")
            nc.sync.dma_start(pick[:], source)
            picks.append(pick)
        og_sb = sb.tile([P, 1], F32, name="og_sb")
        nc.gpsimd.dma_start(out=og_sb[:], in_=og)
        base_sb = sb.tile([P, J], F32, name="base_sb")
        nc.sync.dma_start(out=base_sb[:], in_=base)

        ident = sb.tile([P, P], F32, name="ident")
        make_identity(nc, ident[:])

        windows = []
        for n in range(3):
            window = sb.tile([P, J], F32, name=f"window{n}")
            nc.vector.memset(window[:], 0.0)
            windows.append(window)

        w1_grouped, dst, src = interleave_views(sb, w1_raw, "w1_grouped")
        nc.scalar.activation(dst, src, ACT.Copy, scale=-1.0)
        slot_words = sb.tile([P, J], U16, name="slot_words", align_bytes=64)
        nc.vector.tensor_copy(slot_words[:], table_words[:].indirect(slots[:]))
        w1_codes, w1_scales = quantize(nc, sb, w1_grouped, "w1")
        wo_grouped, dst, src = interleave_views(sb, wo_raw, "wo_grouped")
        nc.scalar.activation(dst, src, ACT.Copy)

        e = sb.tile([P, J], F32, name="e")
        for h in range(2):
            entries = slice(h * HALF_J // GROUP, (h + 1) * HALF_J // GROUP)
            slot_scales = sb.tile([P, HALF_J], U8, name=f"slot_scales{h}", align_bytes=64)
            nc.vector.tensor_copy(slot_scales[:], table_scales[:].indirect(slots[:, entries]))
            for b in range(2 * h, 2 * h + 2):
                cols = slice(b * P, (b + 1) * P)
                a_ps = ps.tile([P, P], F32, name=f"a_ps{b}", tag=f"block{b}")
                nc.tensor.matmul_mx(
                    out=a_ps[:],
                    lhsT=w1_codes[:].bitcast(FP8X4),
                    lhsT_scale=w1_scales[:],
                    rhs=slot_words[:, cols].bitcast(FP4X4),
                    rhs_scale=slot_scales[:, (b % 2) * P : (b % 2 + 1) * P],
                    start=True,
                    stop=True,
                )
                nc.scalar.activation(e[:, cols], a_ps[:], ACT.Exp, scale=temper_sb[:])

        dy_grouped, dst, src = interleave_views(sb, dy_raw, "dy_grouped")
        nc.vector.tensor_copy(dst, src)
        wo_codes, wo_scales = quantize(nc, sb, wo_grouped, "wo")
        dy_codes, dy_scales = quantize(nc, sb, dy_grouped, "dy")
        c0_ps = ps.tile([P, M], F32, name="c0_ps")
        nc.tensor.matmul_mx(
            out=c0_ps[:],
            lhsT=wo_codes[:].bitcast(FP8X4),
            lhsT_scale=wo_scales[:],
            rhs=dy_codes[:].bitcast(FP8X4),
            rhs_scale=dy_scales[:],
            start=True,
            stop=True,
        )

        halves = [
            (slice(h * HALF_M, (h + 1) * HALF_M), slice(h * HALF_M // GROUP, (h + 1) * HALF_M // GROUP))
            for h in range(2)
        ]
        e_picked_all = sb.tile([P, 3 * M], F32, name="e_picked", tag="dy_grouped", align_bytes=64)
        e_picked = [e_picked_all[:, n * M : (n + 1) * M] for n in range(3)]
        s_part = sb.tile([P, M], F32, name="s_part", tag="s_part")
        s = sb.tile([P, M], F32, name="s")
        root = sb.tile([P, M], F32, name="root")
        inv_s = sb.tile([P, M], F32, name="inv_s")
        for n in range(3):
            nc.vector.tensor_copy(e_picked[n], e[:].indirect(picks[n][:]))
        for cols, entries in halves:
            nc.vector.tensor_tensor(s_part[:, cols], e_picked[0][:, cols], e_picked[1][:, cols], ADD)
        for cols, entries in halves:
            nc.vector.tensor_tensor(s[:, cols], s_part[:, cols], e_picked[2][:, cols], ADD)
            nc.scalar.activation(root[:, cols], s[:, cols], ACT.Abs_reciprocal_sqrt)
            nc.scalar.activation(inv_s[:, cols], root[:, cols], ACT.Square)
        c0_e = sb.tile([P, M], F32, name="c0_e", tag="s_part")
        nc.vector.scalar_tensor_tensor(c0_e[:], c0_ps[:], -2.0, e_picked[0], MULT, MULT)

        direct_gain = sb.tile([P, 1], F32, name="direct_gain")
        nc.gpsimd.tensor_scalar(direct_gain[:], og_sb[:], temper_sb[:], -0.5, MULT, MULT)

        def add_on_tensor_engine(addends, name):
            turned = sb.tile([P, J], F32, name=name + "_turned")
            back = [ps.tile([P, HALF_J], F32, name=f"{name}_back{h}", tag=f"half{h}") for h in range(2)]
            blocks = [slice(b * P, (b + 1) * P) for b in range(J // P)]
            sums = [ps.tile([P, P], F32, name=f"{name}_sum{b}", tag=f"block{b}") for b in range(J // P)]
            for n, addend in enumerate(addends):
                for b, cols in enumerate(blocks):
                    nc.tensor.matmul(
                        sums[b][:],
                        addend[:, cols],
                        ident[:],
                        start=(n == 0),
                        stop=(n == len(addends) - 1),
                        is_transpose=True,
                    )
            for b, cols in enumerate(blocks):
                nc.scalar.copy(turned[:, cols], sums[b][:])
                nc.tensor.transpose(back[b // 2][:, (b % 2) * P : (b % 2 + 1) * P], turned[:, cols], ident[:])
            return back

        q = sb.tile([P, M], F32, name="q")
        for h, (cols, entries) in enumerate(halves):
            if h == 1:
                nc.vector.scalar_tensor_tensor(q[:], c0_ps[:], -2.0, inv_s[:], MULT, MULT)
            nc.vector.tensor_tensor(windows[0][:].indirect(picks[0][:, entries]), c0_e[:, cols], inv_s[:, cols], MULT)
        for n in (1, 2):
            nc.vector.tensor_tensor(windows[n][:].indirect(picks[n][:]), q[:], e_picked[n], MULT)
        u = sb.tile([P, M], F32, name="u")
        nc.vector.scalar_tensor_tensor(u[:], q[:], 0.5, inv_s[:], MULT, MULT)

        slot_halves = [slice(h * HALF_J, (h + 1) * HALF_J) for h in range(2)]
        first_two = add_on_tensor_engine(windows[:2], "first")
        neg_hda = sb.tile([P, J], F32, name="neg_hda")
        hde = sb.tile([P, J], F32, name="hde")
        for h, cols in enumerate(slot_halves):
            nc.vector.tensor_tensor(neg_hda[:, cols], first_two[h][:], windows[2][:, cols], ADD)
        for cols in slot_halves:
            nc.vector.scalar_tensor_tensor(hde[:, cols], neg_hda[:, cols], temper_sb[:], e[:, cols], MULT, MULT)

        hda_sq = sb.tile([P, J], F32, name="hda_sq")
        nc.scalar.activation(hda_sq[:], neg_hda[:], ACT.Square)
        direct = sb.tile([P, J], F32, name="direct")
        nc.scalar.activation(direct[:], hda_sq[:], ACT.Copy, scale=direct_gain[:])

        running = [sb.tile([P, M], F32, name=f"hds{n}") for n in range(3)]
        for cols, entries in halves:
            nc.vector.tensor_copy(running[0][:, cols], hde[:].indirect(picks[0][:, entries]))
        for n in (1, 2):
            for cols, entries in halves:
                nc.vector.tensor_tensor(
                    running[n][:, cols], hde[:].indirect(picks[n][:, entries]), running[n - 1][:, cols], ADD
                )
        hs = sb.tile([P, M], F32, name="hs")
        for cols, entries in halves:
            nc.vector.scalar_tensor_tensor(hs[:, cols], running[2][:, cols], og_sb[:], u[:, cols], MULT, MULT)
        for cols, entries in halves:
            nc.vector.tensor_tensor(
                windows[0][:].indirect(picks[0][:, entries]), hs[:, cols], e_picked[0][:, cols], MULT
            )
        for n in (1, 2):
            nc.vector.tensor_tensor(windows[n][:].indirect(picks[n][:]), hs[:], e_picked[n], MULT)

        rest = add_on_tensor_engine((base_sb, direct, windows[0], windows[1]), "last")
        for h, cols in enumerate(slot_halves):
            result = sb.tile([P, HALF_J], F32, name=f"result{h}")
            nc.vector.tensor_tensor(result[:], rest[h][:], windows[2][:, cols], ADD)
            (nc.sync, nc.scalar)[h].dma_start(out=out[:, cols], in_=result[:])
